import numpy as np
import ml_dtypes


def mxq(x, axis, fmt="e4m3"):
    dtype, down = {"e4m3": (ml_dtypes.float8_e4m3fn, 7), "e5m2": (ml_dtypes.float8_e5m2, 14)}[fmt]
    v = np.moveaxis(np.asarray(x, np.float32).astype(ml_dtypes.bfloat16).astype(np.float64), axis, -1)
    blocks = v.reshape(v.shape[:-1] + (-1, 32))
    amax = np.abs(blocks).max(-1, keepdims=True)
    byte = np.maximum(np.where(amax > 0, np.frexp(amax)[1] - 1 + 127, 0) - down, 1)
    scale = np.exp2(byte - 127.0)
    codes = (blocks / scale).astype(np.float32).astype(dtype).astype(np.float64)
    return np.moveaxis((codes * scale).reshape(v.shape), -1, axis)


WIDE = False


def mx_kscale(k):
    if not WIDE:
        return np.ones(k)
    levels = np.array([10, -10, 5, -5, 0])
    if k % 512:
        return np.exp2(np.random.permutation(np.resize(levels, k // 32))).repeat(32)
    a = np.empty((k // 512, 16))
    for p in range(k // 512):
        a[p, :8] = np.random.permutation(np.resize(levels, 8))
        for g in range(8):
            far = levels[np.abs(levels - a[p, g]) >= 10]
            a[p, g + 8] = far[np.random.randint(len(far))]
    return np.exp2(a.ravel()).repeat(32)


def f64(x):
    return np.asarray(x).astype(np.float64)


def striped(idx):
    return np.tile(idx.reshape(-1, 16).T, (8, 1)).astype(np.uint16)


def unstriped(offs):
    return offs[:16].T.reshape(-1).astype(np.int64)


E2M1 = np.array([0.0, 0.5, 1.0, 1.5, 2.0, 3.0, 4.0, 6.0, -0.0, -0.5, -1.0, -1.5, -2.0, -3.0, -4.0, -6.0])


def pack_weight(w, fmt):
    k, n = w.shape
    w = f64(np.asarray(w, np.float32).astype(ml_dtypes.bfloat16)).reshape(k // 32, 32, n)
    amax = np.abs(w).max(1)
    if fmt == "e4m3":
        byte = np.frexp(amax)[1] - 1 + 127 - 7
    else:
        mant, ex = np.frexp(amax / 6.0)
        byte = np.where(mant > 0.5, ex, ex - 1) + 127
    byte = np.clip(np.where(amax > 0, byte, 1), 1, 254)
    scaled = (w * np.exp2(127.0 - byte)[:, None, :]).reshape(k, n).astype(np.float32)
    by_word = np.ascontiguousarray(scaled.reshape(k // 512, 128, 4, n).transpose(0, 1, 3, 2))
    if fmt == "e4m3":
        words = by_word.astype(ml_dtypes.float8_e4m3fn).view(np.uint8)
    else:
        c = by_word.astype(ml_dtypes.float4_e2m1fn).view(np.uint8) & 0xF
        words = (c[..., 0::2] | (c[..., 1::2] << 4)).reshape(k // 512, 128, 2 * n)
    return np.ascontiguousarray(words), np.ascontiguousarray(byte.astype(np.uint8).reshape(k // 512, 16, n))


def unpack_weight(words, scales, fmt):
    g, _, n = scales.shape
    words = np.ascontiguousarray(words).reshape(g, 128, n, -1)
    if fmt == "e4m3":
        vals = words.view(ml_dtypes.float8_e4m3fn).astype(np.float64)
    else:
        nib = np.empty((g, 128, n, 4), np.uint8)
        nib[..., 0::2] = words & 0xF
        nib[..., 1::2] = words >> 4
        vals = E2M1[nib]
    vals = vals * np.repeat(np.exp2(scales.astype(np.float64) - 127.0), 8, axis=1)[..., None]
    return vals.transpose(0, 1, 3, 2).reshape(g * 512, n)


def gelu(v):
    return 0.5 * v * (1.0 + np.tanh(np.sqrt(2.0 / np.pi) * (v + 0.044715 * v**3)))


K, T, S, H, T2, P, N = 1536, 2048, 1024, 512, 2048, 1024, 640

def setup_inputs():
    n = np.random.standard_normal
    s = mx_kscale(K)[:, None]
    u = mx_kscale(H)[:, None]
    d = {}
    d["tab_words"], d["tab_scales"] = pack_weight(n((K, T)) * s, "e4m3")
    d["offs"] = striped(np.random.permutation(T)[:S])
    d["offs2"] = striped(np.random.permutation(T2)[:S])
    d["offs3"] = striped(np.random.permutation(T2)[:P])
    d["offs4"] = striped(np.random.permutation(T2)[:P])
    d["w1"] = (1.5 * n((K, H)) / K ** 0.5 / s).astype(np.float32)
    d["rest"] = n(H).astype(np.float32)
    d["wgs"] = np.exp(0.3 * n((128, S))).astype(np.float32)
    d["page0"] = (2.0 * n((H, T2))).astype(np.float32)
    d["gain"] = (0.5 * np.exp(0.3 * n(H)) * u[:, 0]).astype(np.float32)
    d["w2_words"], d["w2_scales"] = pack_weight(n((H, N)) / H ** 0.5 / u, "e2m1")
    d["w3"] = (n((H, N)) / H ** 0.5 / u).astype(np.float32)
    d["wgo"] = np.exp(0.3 * n((128, P))).astype(np.float32)
    d["page1"] = n((N, T2)).astype(np.float32)
    return d

def reference(tab_words, tab_scales, offs, offs2, offs3, offs4, w1, rest, wgs, page0, gain, w2_words, w2_scales, w3, wgo, page1):
    v = unpack_weight(tab_words, tab_scales, "e4m3")[:, unstriped(offs)]
    dev = (mxq(f64(w1), 0, "e4m3").T @ v) - f64(rest)[:, None]
    h = np.sqrt(np.square(dev) + 1.0)
    page = f64(page0).copy()
    page[:, unstriped(offs2)] = np.tile(f64(wgs), (H // 128, 1)) * h
    x = page[:, unstriped(offs3)] * f64(gain)[:, None]
    xq = mxq(x, 0, "e4m3")
    y1 = unpack_weight(w2_words, w2_scales, "e2m1").T @ xq
    y2 = mxq(f64(w3), 0, "e4m3").T @ xq
    y = y1 * y2 + y1
    out = f64(page1).copy()
    out[:, unstriped(offs4)] = np.tile(f64(wgo), (N // 128, 1)) * y
    return out

@@ -1,0 +1,286 @@
+from contextlib import ExitStack
+
+import concourse.mybir as mybir
+from concourse.masks import make_identity
+
+K, T, S, H, N = 1536, 2048, 1024, 512, 640
+FLOPS = 2 * K * H * S + 2 * 2 * H * N * S
+
+F32 = mybir.dt.float32
+BF16 = mybir.dt.bfloat16
+I32 = mybir.dt.int32
+U32 = mybir.dt.uint32
+U16 = mybir.dt.uint16
+U8 = mybir.dt.uint8
+FP8X4 = mybir.dt.float8_e4m3fn_x4
+FP4X4 = mybir.dt.float4_e2m1fn_x4
+ACT = mybir.ActivationFunctionType
+ALU = mybir.AluOpType
+
+P = 128
+PASSES = K // 512
+HALF = S // 2
+FIRST = 256
+REST = S - FIRST
+H_TILES = H // P
+N_TILES = N // P
+
+
+def tile_list_saddle_reflocking_page_kernel(
+    tc, tab_words, tab_scales, offs, offs2, offs3, offs4, w1, rest, wgs, page0, gain,
+    w2_words, w2_scales, w3, wgo, page1, out,
+):
+    nc = tc.nc
+    with ExitStack() as ctx:
+        lists = ctx.enter_context(tc.tile_pool(name="lists", bufs=1))
+        keep = ctx.enter_context(tc.tile_pool(name="keep", bufs=1))
+        ring = ctx.enter_context(tc.tile_pool(name="ring", bufs=2))
+        psum = ctx.enter_context(tc.psum_pool(name="psum", bufs=8))
+
+        def load_list(src, name):
+            tile = lists.tile([P, S // 16], U16, name=name)
+            nc.sync.dma_start(tile[:], src)
+            return tile
+
+        def entries(tile, start, count):
+            return tile[:, start // 16 : (start + count) // 16]
+
+        def load_table_pass(a):
+            tile = keep.tile([P, T], U32, name="tab_w%d" % a)
+            nc.sync.dma_start(tile[:].bitcast(I32), tab_words[a].rearrange("p t i -> p (t i)").bitcast(I32))
+            return tile
+
+        def load_weight(src, row0, col0, width):
+            raw = ring.tile([P, 4, width], F32, name="raw", tag="raw", bufs=3)
+            nc.sync.dma_start(raw[:], src[row0 : row0 + 512, col0 : col0 + width].rearrange("(p i) c -> p i c", i=4))
+            return raw
+
+        def quantize_weight(raw, width, name):
+            grouped = ring.tile([P, width, 4], BF16, name="w_bf", tag="w_bf", bufs=3, align_bytes=64)
+            nc.scalar.copy(
+                out=grouped[:].rearrange("p (c j) i -> p c i j", j=4),
+                in_=raw[:].rearrange("p i (c j) -> p c i j", j=4),
+            )
+            codes = keep.tile([P, width], U32, name=name + "_c", align_bytes=64)
+            scales = keep.tile([P, width], U8, name=name + "_s", align_bytes=64)
+            nc.vector.quantize_mx(
+                out=codes[:].bitcast(FP8X4), scales=scales[:], in_=grouped[:].rearrange("p c i -> p (c i)")
+            )
+            return codes, scales
+
+        def load_rows(src, u, name):
+            tile = keep.tile([P, T], F32, name="%s%d" % (name, u))
+            nc.sync.dma_start(tile[:], src[u * P : (u + 1) * P, :])
+            return tile
+
+        def load_cols(src, start, count, name):
+            tile = keep.tile([P, count], F32, name=name)
+            nc.sync.dma_start(tile[:], src[:, start : start + count])
+            return tile
+
+        tab_s = keep.tile([P, T], U8, name="tab_s")
+        nc.vector.memset(tab_s[:].bitcast(I32), 0)
+        w2_s = keep.tile([P, N], U8, name="w2_s", align_bytes=64)
+        nc.vector.memset(w2_s[:].bitcast(I32), 0)
+        list1 = load_list(offs, "list1")
+        tab_w = [load_table_pass(0)]
+        for q in range(4):
+            nc.scalar.dma_start(
+                tab_s[32 * q : 32 * q + 4 * PASSES, :].bitcast(I32), tab_scales[:, 4 * q : 4 * q + 4, :].bitcast(I32)
+            )
+        rest_t = keep.tile([P, H_TILES], F32, name="rest_t")
+        gain_t = keep.tile([P, H_TILES], F32, name="gain_t")
+        with nc.allow_non_contiguous_dma(reason="one value a partition"):
+            nc.scalar.dma_start(rest_t[:], rest.rearrange("(u p) -> p u", p=P))
+            nc.scalar.dma_start(gain_t[:], gain.rearrange("(u p) -> p u", p=P))
+        w1_raw = [load_weight(w1, 512 * a, 0, 256) for a in range(PASSES)]
+        tab_w.extend(load_table_pass(a) for a in range(1, PASSES))
+        list2 = load_list(offs2, "list2")
+        wgs_t = keep.tile([P, S], F32, name="wgs_t", tag="hold_c")
+        nc.sync.dma_start(wgs_t[:, 0:HALF], wgs[:, 0:HALF])
+        pages = [load_rows(page0, 0, "page0_")]
+        nc.sync.dma_start(wgs_t[:, HALF:S], wgs[:, HALF:S])
+
+        ident_bf = keep.tile([P, P], BF16, name="ident_bf")
+        make_identity(nc, ident_bf[:])
+        ident_f32 = keep.tile([P, P], F32, name="ident_f32")
+        make_identity(nc, ident_f32[:])
+
+        got_w = [keep.tile([P, S], U32, name="got_w%d" % a, align_bytes=64) for a in range(PASSES)]
+        got_s = keep.tile([P, S], U8, name="got_s", align_bytes=64)
+        nc.vector.tensor_copy(got_w[0][:], tab_w[0][:].indirect(list1[:]))
+        nc.vector.tensor_copy(got_s[:], tab_s[:].indirect(list1[:]))
+        w1_q = [[quantize_weight(w1_raw[a], 256, "w1_0%d" % a) for a in range(PASSES)]]
+        nc.vector.tensor_copy(got_w[1][:], tab_w[1][:].indirect(list1[:]))
+        for half in range(2):
+            nc.vector.tensor_copy(
+                got_w[2][:, half * HALF : (half + 1) * HALF], tab_w[2][:].indirect(entries(list1, half * HALF, HALF))
+            )
+
+        w1_raw = [load_weight(w1, 512 * a, 256, 256) for a in range(PASSES)]
+        list3 = load_list(offs3, "list3")
+        pages.append(load_rows(page0, 1, "page0_"))
+
+        def first_stage(u, half, h):
+            cols = slice(half * HALF, (half + 1) * HALF)
+            rows = slice((u % 2) * P, (u % 2 + 1) * P)
+            acc = psum.tile([P, HALF], F32, name="acc", tag="bank")
+            for a in range(PASSES):
+                codes, scales = w1_q[u // 2][a]
+                nc.tensor.matmul_mx(
+                    out=acc[:], lhsT=codes[:, rows].bitcast(FP8X4), lhsT_scale=scales[:, rows],
+                    rhs=got_w[a][:, cols].bitcast(FP8X4), rhs_scale=got_s[4 * a : P, cols],
+                    start=(a == 0), stop=(a == PASSES - 1),
+                )
+            square = ring.tile([P, HALF], F32, name="square", tag="square")
+            nc.scalar.activation(out=square[:], in_=acc[:], func=ACT.Square, bias=rest_t[:, u : u + 1], scale=-1.0)
+            nc.scalar.activation(out=h[:, cols], in_=square[:], func=ACT.Sqrt, bias=1.0)
+
+        def replace(u, h, start, count):
+            cols = slice(start, start + count)
+            nc.vector.tensor_tensor(
+                pages[u][:].indirect(entries(list2, start, count)), h[:, cols], wgs_t[:, cols], ALU.mult
+            )
+
+        def turn_in(picked, u, blocks, x_bf, x_t):
+            nc.scalar.activation(out=x_bf, in_=picked, func=ACT.Copy, scale=gain_t[:, u : u + 1])
+            turned = psum.tile([P, blocks, P], BF16, name="turned", tag="bank")
+            for b in range(blocks):
+                nc.tensor.transpose(turned[:, b, :], x_bf[:, b * P : (b + 1) * P], ident_bf[:])
+            nc.scalar.copy(out=x_t[:, :, u * P : (u + 1) * P], in_=turned[:])
+
+        def turn_back(x_t, b0, grouped, g0):
+            words = x_t[:].bitcast(F32)
+            back = psum.tile([P, 2, 2, P], F32, name="back", tag="bank")
+            for b in range(2):
+                for e in range(2):
+                    nc.tensor.transpose(back[:, b, e, :], words[:, b0 + b, e : 2 * P : 2], ident_f32[:])
+            nc.scalar.copy(
+                out=grouped[:].bitcast(F32)[:, g0 * 2 : (g0 + 256) * 2].rearrange("p (b j e) -> p b j e", b=2, e=2),
+                in_=back[:].rearrange("p b e j -> p b j e"),
+            )
+
+        def quantize_x(grouped, width, name):
+            codes = keep.tile([P, width], U32, name=name + "_c", align_bytes=64)
+            scales = keep.tile([P, width], U8, name=name + "_s", align_bytes=64)
+            nc.vector.quantize_mx(out=codes[:].bitcast(FP8X4), scales=scales[:], in_=grouped[:])
+            return codes, scales
+
+        hs = [
+            keep.tile([P, S], F32, name="h%d" % u, tag="hold_a" if u == H_TILES - 1 else "h%d" % u)
+            for u in range(H_TILES)
+        ]
+        for half in range(2):
+            first_stage(0, half, hs[0])
+            replace(0, hs[0], half * HALF, HALF)
+        for half in range(2):
+            first_stage(1, half, hs[1])
+        w1_q.append([quantize_weight(w1_raw[a], 256, "w1_1%d" % a) for a in range(PASSES)])
+        w3_cols = [(0, 256), (256, 256), (512, 128)]
+        pages.append(load_rows(page0, 2, "page0_"))
+        w3_raw = [load_weight(w3, 0, c0, width) for c0, width in w3_cols]
+        pages.append(load_rows(page0, 3, "page0_"))
+        w2_w = keep.tile([P, 2 * N], U8, name="w2_w", align_bytes=64)
+        nc.sync.dma_start(w2_w[:].bitcast(I32), w2_words[0].bitcast(I32))
+        for q in range(4):
+            nc.sync.dma_start(
+                w2_s[32 * q : 32 * q + 4, :].bitcast(I32), w2_scales[0, 4 * q : 4 * q + 4, :].bitcast(I32)
+            )
+        list4 = load_list(offs4, "list4")
+        wgo_t = load_cols(wgo, 0, S, "wgo_t")
+        outs = [load_rows(page1, n, "page1_") for n in range(N_TILES)]
+
+        replace(1, hs[1], 0, S)
+        for u in range(2, H_TILES):
+            for half in range(2):
+                first_stage(u, half, hs[u])
+        replace(2, hs[2], 0, S)
+        w3_q = [quantize_weight(w3_raw[i], w3_cols[i][1], "w3_%d" % i) for i in range(len(w3_cols))]
+        replace(3, hs[3], 0, S)
+
+        picked_first = keep.tile([P, H_TILES, FIRST], F32, name="picked_first", tag="hold_a")
+        x_t_first = keep.tile([P, FIRST // P, H], BF16, name="x_t_first", tag="hold_d")
+        for u in range(H_TILES):
+            nc.vector.tensor_copy(picked_first[:, u, :], pages[u][:].indirect(entries(list3, 0, FIRST)))
+            x_bf = ring.tile([P, FIRST], BF16, name="x_bf", tag="x_bf")
+            turn_in(picked_first[:, u, :], u, FIRST // P, x_bf[:], x_t_first)
+        grouped_first = keep.tile([P, 4 * FIRST], BF16, name="grouped_first", tag="hold_b", align_bytes=64)
+        turn_back(x_t_first, 0, grouped_first, 0)
+
+        def pick_rest(u0, tag, align):
+            picked = keep.tile([P, 2, REST], F32, name="picked_rest%d" % u0, tag=tag, align_bytes=align)
+            for i in range(2):
+                nc.vector.tensor_copy(picked[:, i, :], pages[u0 + i][:].indirect(entries(list3, FIRST, REST)))
+            return [picked[:, i, :] for i in range(2)]
+
+        picked_rest = pick_rest(0, "hold_c", None)
+        x_first = quantize_x(grouped_first, FIRST, "x_first")
+        picked_rest.extend(pick_rest(2, "hold_b", 64))
+
+        def products(n, x_q, width, y1_acc, y2_acc, dst):
+            codes, scales = x_q
+            w3_codes, w3_scales = w3_q[n // 2]
+            rows = slice((n % 2) * P, (n % 2 + 1) * P)
+            nc.tensor.matmul_mx(
+                out=y1_acc, lhsT=w2_w[:, 2 * n * P : 2 * (n + 1) * P].bitcast(FP4X4),
+                lhsT_scale=w2_s[:, n * P : (n + 1) * P],
+                rhs=codes[:].bitcast(FP8X4), rhs_scale=scales[:], start=True, stop=True,
+            )
+            nc.tensor.matmul_mx(
+                out=y2_acc, lhsT=w3_codes[:, rows].bitcast(FP8X4), lhsT_scale=w3_scales[:, rows],
+                rhs=codes[:].bitcast(FP8X4), rhs_scale=scales[:], start=True, stop=True,
+            )
+            y1 = ring.tile([P, width], F32, name="y1", tag="y1_%d" % width, bufs=3 if width == 256 else 2)
+            nc.scalar.copy(out=y1[:], in_=y1_acc)
+            nc.vector.scalar_tensor_tensor(out=dst, in0=y2_acc, scalar=1.0, in1=y1[:], op0=ALU.add, op1=ALU.mult)
+
+        def narrow_products(n, x_q, dst):
+            acc = psum.tile([P, 2, 256], F32, name="y_acc", tag="bank")
+            products(n, x_q, 256, acc[:, 0, :], acc[:, 1, :], dst)
+
+        def wide_products(n, x_q, dst):
+            acc1 = psum.tile([P, 512], F32, name="y1_acc", tag="bank")
+            acc2 = psum.tile([P, 512], F32, name="y2_acc", tag="bank")
+            products(n, x_q, 512, acc1[:], acc2[:], dst)
+
+        def put(n, y, start, count):
+            nc.vector.tensor_tensor(
+                outs[n][:].indirect(entries(list4, start, count)), y[:], wgo_t[:, start : start + count], ALU.mult
+            )
+
+        def first_scores(n):
+            y = ring.tile([P, FIRST], F32, name="y_first", tag="y_first", bufs=3)
+            narrow_products(n, x_first, y[:])
+            return y
+
+        ys = [first_scores(0), first_scores(1)]
+        x_t_rest = keep.tile([P, REST // P, H], BF16, name="x_t_rest")
+        x_bf_rest = keep.tile([P, H_TILES, REST], BF16, name="x_bf_rest", tag="hold_d")
+        for u in range(H_TILES):
+            turn_in(picked_rest[u], u, REST // P, x_bf_rest[:, u, :], x_t_rest)
+        grouped_mid = keep.tile([P, 4 * 256], BF16, name="grouped_mid", align_bytes=64)
+        grouped_end = keep.tile([P, 4 * 512], BF16, name="grouped_end", align_bytes=64)
+        turn_back(x_t_rest, 0, grouped_mid, 0)
+        turn_back(x_t_rest, 2, grouped_end, 0)
+        turn_back(x_t_rest, 4, grouped_end, 256)
+        for n in range(N_TILES - 1):
+            put(n, ys[n], 0, FIRST)
+            if n + 2 < N_TILES:
+                ys.append(first_scores(n + 2))
+            if n == 1:
+                x_mid = quantize_x(grouped_mid, 256, "x_mid")
+                x_end = quantize_x(grouped_end, 512, "x_end")
+
+        def rest_scores(n):
+            y = ring.tile([P, REST], F32, name="y_rest", tag="y_rest")
+            narrow_products(n, x_mid, y[:, 0:256])
+            wide_products(n, x_end, y[:, 256:REST])
+            return y
+
+        zs = [rest_scores(0)]
+        put(N_TILES - 1, ys[N_TILES - 1], 0, FIRST)
+        for n in range(N_TILES):
+            if n + 1 < N_TILES:
+                zs.append(rest_scores(n + 1))
+            put(n, zs[n], FIRST, REST)
+            nc.sync.dma_start(out[n * P : (n + 1) * P, :], outs[n][:])

@@ -105,6 +105,8 @@ def tile_list_saddle_reflocking_page_kernel(
         make_identity(nc, ident_bf[:])
         ident_f32 = keep.tile([P, P], F32, name="ident_f32")
         make_identity(nc, ident_f32[:])
+        warm = keep.tile([P, 1], F32, name="warm")
+        nc.scalar.activation(out=warm[:], in_=ident_f32[:, 0:1], func=ACT.Sqrt, bias=1.0)
 
         got_w = [keep.tile([P, S], U32, name="got_w%d" % a, align_bytes=64) for a in range(PASSES)]
         got_s = keep.tile([P, S], U8, name="got_s", align_bytes=64)

@@ -35,7 +35,8 @@ def tile_list_saddle_reflocking_page_kernel(
         lists = ctx.enter_context(tc.tile_pool(name="lists", bufs=1))
         keep = ctx.enter_context(tc.tile_pool(name="keep", bufs=1))
         ring = ctx.enter_context(tc.tile_pool(name="ring", bufs=2))
-        psum = ctx.enter_context(tc.psum_pool(name="psum", bufs=8))
+        psum = ctx.enter_context(tc.psum_pool(name="psum", bufs=6))
+        side = ctx.enter_context(tc.psum_pool(name="side", bufs=2))
 
         def load_list(src, name):
             tile = lists.tile([P, S // 16], U16, name=name)
@@ -59,7 +60,7 @@ def tile_list_saddle_reflocking_page_kernel(
             grouped = ring.tile([P, width, 4], BF16, name="w_bf", tag="w_bf", bufs=3, align_bytes=64)
             nc.scalar.copy(
                 out=grouped[:].rearrange("p (c j) i -> p c i j", j=4),
-                in_=raw[:].rearrange("p i (c j) -> p c i j", j=4),
+                in_=raw[:, :, 0:width].rearrange("p i (c j) -> p c i j", j=4),
             )
             codes = keep.tile([P, width], U32, name=name + "_c", align_bytes=64)
             scales = keep.tile([P, width], U8, name=name + "_s", align_bytes=64)
@@ -67,6 +68,20 @@ def tile_list_saddle_reflocking_page_kernel(
                 out=codes[:].bitcast(FP8X4), scales=scales[:], in_=grouped[:].rearrange("p c i -> p (c i)")
             )
             return codes, scales
+
+        def quantize_w1(raws, u):
+            grouped = ring.tile([P, PASSES, P, 4], BF16, name="w1_bf", tag="w_bf", bufs=3, align_bytes=64)
+            for a in range(PASSES):
+                nc.scalar.copy(
+                    out=grouped[:, a].rearrange("p (c j) i -> p c i j", j=4),
+                    in_=raws[a][:, :, (u % 2) * P : (u % 2 + 1) * P].rearrange("p i (c j) -> p c i j", j=4),
+                )
+            codes = keep.tile([P, PASSES * P], U32, name="w1_c%d" % u, align_bytes=64)
+            scales = keep.tile([P, PASSES * P], U8, name="w1_s%d" % u, align_bytes=64)
+            nc.vector.quantize_mx(
+                out=codes[:].bitcast(FP8X4), scales=scales[:], in_=grouped[:].rearrange("p a c i -> p (a c i)")
+            )
+            return [(codes[:, a * P : (a + 1) * P], scales[:, a * P : (a + 1) * P]) for a in range(PASSES)]
 
         def load_rows(src, u, name):
             tile = keep.tile([P, T], F32, name="%s%d" % (name, u))
@@ -85,16 +100,15 @@ def tile_list_saddle_reflocking_page_kernel(
         list1 = load_list(offs, "list1")
         tab_w = [load_table_pass(0)]
         for q in range(4):
-            nc.scalar.dma_start(
+            nc.sync.dma_start(
                 tab_s[32 * q : 32 * q + 4 * PASSES, :].bitcast(I32), tab_scales[:, 4 * q : 4 * q + 4, :].bitcast(I32)
             )
-        rest_t = keep.tile([P, H_TILES], F32, name="rest_t")
-        gain_t = keep.tile([P, H_TILES], F32, name="gain_t")
-        with nc.allow_non_contiguous_dma(reason="one value a partition"):
-            nc.scalar.dma_start(rest_t[:], rest.rearrange("(u p) -> p u", p=P))
-            nc.scalar.dma_start(gain_t[:], gain.rearrange("(u p) -> p u", p=P))
-        w1_raw = [load_weight(w1, 512 * a, 0, 256) for a in range(PASSES)]
+        vectors = keep.tile([P, P], F32, name="vectors")
+        nc.gpsimd.memset(vectors[:], 0.0)
+        nc.scalar.dma_start(vectors[0:H_TILES, :], rest.rearrange("(u p) -> u p", p=P))
+        nc.scalar.dma_start(vectors[H_TILES : 2 * H_TILES, :], gain.rearrange("(u p) -> u p", p=P))
         tab_w.extend(load_table_pass(a) for a in range(1, PASSES))
+        w1_raw = [load_weight(w1, 512 * a, 0, 256) for a in range(PASSES)]
         list2 = load_list(offs2, "list2")
         wgs_t = keep.tile([P, S], F32, name="wgs_t", tag="hold_c")
         nc.sync.dma_start(wgs_t[:, 0:HALF], wgs[:, 0:HALF])
@@ -108,34 +122,35 @@ def tile_list_saddle_reflocking_page_kernel(
         warm = keep.tile([P, 1], F32, name="warm")
         nc.scalar.activation(out=warm[:], in_=ident_f32[:, 0:1], func=ACT.Sqrt, bias=1.0)
 
+        turned_vectors = psum.tile([P, P], F32, name="turned_vectors", tag="bank")
+        nc.tensor.transpose(turned_vectors[:], vectors[:], ident_f32[:])
+        per_row = keep.tile([P, 2 * H_TILES], F32, name="per_row")
+        nc.scalar.copy(out=per_row[:], in_=turned_vectors[:, 0 : 2 * H_TILES])
+
         got_w = [keep.tile([P, S], U32, name="got_w%d" % a, align_bytes=64) for a in range(PASSES)]
         got_s = keep.tile([P, S], U8, name="got_s", align_bytes=64)
-        nc.vector.tensor_copy(got_w[0][:], tab_w[0][:].indirect(list1[:]))
+        for a in range(PASSES):
+            nc.vector.tensor_copy(got_w[a][:], tab_w[a][:].indirect(list1[:]))
         nc.vector.tensor_copy(got_s[:], tab_s[:].indirect(list1[:]))
-        w1_q = [[quantize_weight(w1_raw[a], 256, "w1_0%d" % a) for a in range(PASSES)]]
-        nc.vector.tensor_copy(got_w[1][:], tab_w[1][:].indirect(list1[:]))
-        for half in range(2):
-            nc.vector.tensor_copy(
-                got_w[2][:, half * HALF : (half + 1) * HALF], tab_w[2][:].indirect(entries(list1, half * HALF, HALF))
-            )
+        by_pass = [quantize_weight(w1_raw[a], P, "w1_first%d" % a) for a in range(PASSES)]
+        w1_q = [[(codes[:], scales[:]) for codes, scales in by_pass], quantize_w1(w1_raw, 1)]
 
         w1_raw = [load_weight(w1, 512 * a, 256, 256) for a in range(PASSES)]
         list3 = load_list(offs3, "list3")
         pages.append(load_rows(page0, 1, "page0_"))
 
-        def first_stage(u, half, h):
-            cols = slice(half * HALF, (half + 1) * HALF)
-            rows = slice((u % 2) * P, (u % 2 + 1) * P)
-            acc = psum.tile([P, HALF], F32, name="acc", tag="bank")
+        def first_stage(u, start, count, h):
+            cols = slice(start, start + count)
+            acc = side.tile([P, count], F32, name="acc", tag="side")
             for a in range(PASSES):
-                codes, scales = w1_q[u // 2][a]
+                codes, scales = w1_q[u][a]
                 nc.tensor.matmul_mx(
-                    out=acc[:], lhsT=codes[:, rows].bitcast(FP8X4), lhsT_scale=scales[:, rows],
+                    out=acc[:], lhsT=codes.bitcast(FP8X4), lhsT_scale=scales,
                     rhs=got_w[a][:, cols].bitcast(FP8X4), rhs_scale=got_s[4 * a : P, cols],
                     start=(a == 0), stop=(a == PASSES - 1),
                 )
-            square = ring.tile([P, HALF], F32, name="square", tag="square")
-            nc.scalar.activation(out=square[:], in_=acc[:], func=ACT.Square, bias=rest_t[:, u : u + 1], scale=-1.0)
+            square = ring.tile([P, count], F32, name="square", tag="square")
+            nc.scalar.activation(out=square[:], in_=acc[:], func=ACT.Square, bias=per_row[:, u : u + 1], scale=-1.0)
             nc.scalar.activation(out=h[:, cols], in_=square[:], func=ACT.Sqrt, bias=1.0)
 
         def replace(u, h, start, count):
@@ -145,15 +160,15 @@ def tile_list_saddle_reflocking_page_kernel(
             )
 
         def turn_in(picked, u, blocks, x_bf, x_t):
-            nc.scalar.activation(out=x_bf, in_=picked, func=ACT.Copy, scale=gain_t[:, u : u + 1])
-            turned = psum.tile([P, blocks, P], BF16, name="turned", tag="bank")
+            nc.scalar.activation(out=x_bf, in_=picked, func=ACT.Copy, scale=per_row[:, H_TILES + u : H_TILES + u + 1])
+            turned = side.tile([P, blocks, P], BF16, name="turned", tag="side")
             for b in range(blocks):
                 nc.tensor.transpose(turned[:, b, :], x_bf[:, b * P : (b + 1) * P], ident_bf[:])
             nc.scalar.copy(out=x_t[:, :, u * P : (u + 1) * P], in_=turned[:])
 
         def turn_back(x_t, b0, grouped, g0):
             words = x_t[:].bitcast(F32)
-            back = psum.tile([P, 2, 2, P], F32, name="back", tag="bank")
+            back = side.tile([P, 2, 2, P], F32, name="back", tag="side")
             for b in range(2):
                 for e in range(2):
                     nc.tensor.transpose(back[:, b, e, :], words[:, b0 + b, e : 2 * P : 2], ident_f32[:])
@@ -163,7 +178,7 @@ def tile_list_saddle_reflocking_page_kernel(
             )
 
         def quantize_x(grouped, width, name):
-            codes = keep.tile([P, width], U32, name=name + "_c", align_bytes=64)
+            codes = keep.tile([P, width], U32, name=name + "_c", tag=name, align_bytes=64)
             scales = keep.tile([P, width], U8, name=name + "_s", align_bytes=64)
             nc.vector.quantize_mx(out=codes[:].bitcast(FP8X4), scales=scales[:], in_=grouped[:])
             return codes, scales
@@ -172,12 +187,12 @@ def tile_list_saddle_reflocking_page_kernel(
             keep.tile([P, S], F32, name="h%d" % u, tag="hold_a" if u == H_TILES - 1 else "h%d" % u)
             for u in range(H_TILES)
         ]
+        for start, count in ((0, 256), (256, 256), (HALF, HALF)):
+            first_stage(0, start, count, hs[0])
+            replace(0, hs[0], start, count)
         for half in range(2):
-            first_stage(0, half, hs[0])
-            replace(0, hs[0], half * HALF, HALF)
-        for half in range(2):
-            first_stage(1, half, hs[1])
-        w1_q.append([quantize_weight(w1_raw[a], 256, "w1_1%d" % a) for a in range(PASSES)])
+            first_stage(1, half * HALF, HALF, hs[1])
+        w1_q.extend(quantize_w1(w1_raw, u) for u in range(2, H_TILES))
         w3_cols = [(0, 256), (256, 256), (512, 128)]
         pages.append(load_rows(page0, 2, "page0_"))
         w3_raw = [load_weight(w3, 0, c0, width) for c0, width in w3_cols]
@@ -195,7 +210,7 @@ def tile_list_saddle_reflocking_page_kernel(
         replace(1, hs[1], 0, S)
         for u in range(2, H_TILES):
             for half in range(2):
-                first_stage(u, half, hs[u])
+                first_stage(u, half * HALF, HALF, hs[u])
         replace(2, hs[2], 0, S)
         w3_q = [quantize_weight(w3_raw[i], w3_cols[i][1], "w3_%d" % i) for i in range(len(w3_cols))]
         replace(3, hs[3], 0, S)
@@ -219,7 +234,7 @@ def tile_list_saddle_reflocking_page_kernel(
         x_first = quantize_x(grouped_first, FIRST, "x_first")
         picked_rest.extend(pick_rest(2, "hold_b", 64))
 
-        def products(n, x_q, width, y1_acc, y2_acc, dst):
+        def products(n, x_q, y1_acc, y2_acc, y1, y2):
             codes, scales = x_q
             w3_codes, w3_scales = w3_q[n // 2]
             rows = slice((n % 2) * P, (n % 2 + 1) * P)
@@ -232,57 +247,66 @@ def tile_list_saddle_reflocking_page_kernel(
                 out=y2_acc, lhsT=w3_codes[:, rows].bitcast(FP8X4), lhsT_scale=w3_scales[:, rows],
                 rhs=codes[:].bitcast(FP8X4), rhs_scale=scales[:], start=True, stop=True,
             )
-            y1 = ring.tile([P, width], F32, name="y1", tag="y1_%d" % width, bufs=3 if width == 256 else 2)
-            nc.scalar.copy(out=y1[:], in_=y1_acc)
-            nc.vector.scalar_tensor_tensor(out=dst, in0=y2_acc, scalar=1.0, in1=y1[:], op0=ALU.add, op1=ALU.mult)
+            nc.scalar.copy(out=y1, in_=y1_acc)
+            nc.scalar.activation(out=y2, in_=y2_acc, func=ACT.Identity, bias=1.0)
 
-        def narrow_products(n, x_q, dst):
+        def narrow_products(n, x_q, y1, y2):
             acc = psum.tile([P, 2, 256], F32, name="y_acc", tag="bank")
-            products(n, x_q, 256, acc[:, 0, :], acc[:, 1, :], dst)
+            products(n, x_q, acc[:, 0, :], acc[:, 1, :], y1, y2)
 
-        def wide_products(n, x_q, dst):
+        def wide_products(n, x_q, y1, y2):
             acc1 = psum.tile([P, 512], F32, name="y1_acc", tag="bank")
             acc2 = psum.tile([P, 512], F32, name="y2_acc", tag="bank")
-            products(n, x_q, 512, acc1[:], acc2[:], dst)
+            products(n, x_q, acc1[:], acc2[:], y1, y2)
+
+        def combine(y1, y2, start, count):
+            nc.gpsimd.tensor_tensor(y1, y1, wgo_t[:, start : start + count], ALU.mult)
+            nc.gpsimd.tensor_tensor(y2, y1, y2, ALU.mult)
 
         def put(n, y, start, count):
-            nc.vector.tensor_tensor(
-                outs[n][:].indirect(entries(list4, start, count)), y[:], wgo_t[:, start : start + count], ALU.mult
-            )
+            nc.vector.tensor_copy(outs[n][:].indirect(entries(list4, start, count)), y[:])
 
-        def first_scores(n):
-            y = ring.tile([P, FIRST], F32, name="y_first", tag="y_first", bufs=3)
-            narrow_products(n, x_first, y[:])
-            return y
+        def scores(n, x_q, start, y1, tag):
+            y2 = keep.tile([P, 256], F32, name="y2", tag=tag, align_bytes=64)
+            narrow_products(n, x_q, y1, y2[:])
+            combine(y1, y2[:], start, 256)
+            return y2
 
-        ys = [first_scores(0), first_scores(1)]
-        x_t_rest = keep.tile([P, REST // P, H], BF16, name="x_t_rest")
+        def wide_scores(n, x_q):
+            y1 = ring.tile([P, HALF], F32, name="y1_wide", tag="raw", bufs=3)
+            y2 = ring.tile([P, HALF], F32, name="y2_wide", tag="y2_wide", bufs=3)
+            wide_products(n, x_q, y1[:], y2[:])
+            combine(y1[:], y2[:], HALF, HALF)
+            return y2
+
+        y1_first = keep.tile([P, N_TILES, 256], F32, name="y1_first", tag="h0")
+        y1_mid = keep.tile([P, N_TILES, 256], F32, name="y1_mid", tag="h1")
+
+        ys = [scores(n, x_first, 0, y1_first[:, n, :], ("first0", "x_mid")[n]) for n in range(2)]
         x_bf_rest = keep.tile([P, H_TILES, REST], BF16, name="x_bf_rest", tag="hold_d")
+        x_t_mid = keep.tile([P, 2, H], BF16, name="x_t_mid")
         for u in range(H_TILES):
-            turn_in(picked_rest[u], u, REST // P, x_bf_rest[:, u, :], x_t_rest)
+            turn_in(picked_rest[u][:, 0:256], u, 2, x_bf_rest[:, u, 0:256], x_t_mid)
         grouped_mid = keep.tile([P, 4 * 256], BF16, name="grouped_mid", align_bytes=64)
-        grouped_end = keep.tile([P, 4 * 512], BF16, name="grouped_end", align_bytes=64)
-        turn_back(x_t_rest, 0, grouped_mid, 0)
-        turn_back(x_t_rest, 2, grouped_end, 0)
-        turn_back(x_t_rest, 4, grouped_end, 256)
-        for n in range(N_TILES - 1):
+        turn_back(x_t_mid, 0, grouped_mid, 0)
+        ys.extend(scores(n, x_first, 0, y1_first[:, n, :], "first%d" % n) for n in range(2, N_TILES))
+        for n in range(2):
             put(n, ys[n], 0, FIRST)
-            if n + 2 < N_TILES:
-                ys.append(first_scores(n + 2))
-            if n == 1:
-                x_mid = quantize_x(grouped_mid, 256, "x_mid")
-                x_end = quantize_x(grouped_end, 512, "x_end")
-
-        def rest_scores(n):
-            y = ring.tile([P, REST], F32, name="y_rest", tag="y_rest")
-            narrow_products(n, x_mid, y[:, 0:256])
-            wide_products(n, x_end, y[:, 256:REST])
-            return y
-
-        zs = [rest_scores(0)]
-        put(N_TILES - 1, ys[N_TILES - 1], 0, FIRST)
+        x_mid = quantize_x(grouped_mid, 256, "x_mid")
+        for n in range(2, N_TILES):
+            put(n, ys[n], 0, FIRST)
+        ys = [scores(n, x_mid, FIRST, y1_mid[:, n, :], ("x_end", "mid1")[n]) for n in range(2)]
+        x_t_end = keep.tile([P, 4, H], BF16, name="x_t_end")
+        for u in range(H_TILES):
+            turn_in(picked_rest[u][:, 256:REST], u, 4, x_bf_rest[:, u, 256:REST], x_t_end)
+        grouped_end = keep.tile([P, 4 * 512], BF16, name="grouped_end", align_bytes=64)
+        turn_back(x_t_end, 0, grouped_end, 0)
+        turn_back(x_t_end, 2, grouped_end, 256)
+        ys.extend(scores(n, x_mid, FIRST, y1_mid[:, n, :], "mid%d" % n) for n in range(2, N_TILES))
+        put(0, ys[0], FIRST, 256)
+        x_end = quantize_x(grouped_end, HALF, "x_end")
+        for n in range(1, N_TILES):
+            put(n, ys[n], FIRST, 256)
         for n in range(N_TILES):
-            if n + 1 < N_TILES:
-                zs.append(rest_scores(n + 1))
-            put(n, zs[n], FIRST, REST)
+            put(n, wide_scores(n, x_end), HALF, HALF)
             nc.sync.dma_start(out[n * P : (n + 1) * P, :], outs[n][:])

@@ -100,7 +100,7 @@ def tile_list_saddle_reflocking_page_kernel(
         list1 = load_list(offs, "list1")
         tab_w = [load_table_pass(0)]
         for q in range(4):
-            nc.sync.dma_start(
+            nc.scalar.dma_start(
                 tab_s[32 * q : 32 * q + 4 * PASSES, :].bitcast(I32), tab_scales[:, 4 * q : 4 * q + 4, :].bitcast(I32)
             )
         vectors = keep.tile([P, P], F32, name="vectors")
@@ -111,9 +111,9 @@ def tile_list_saddle_reflocking_page_kernel(
         w1_raw = [load_weight(w1, 512 * a, 0, 256) for a in range(PASSES)]
         list2 = load_list(offs2, "list2")
         wgs_t = keep.tile([P, S], F32, name="wgs_t", tag="hold_c")
-        nc.sync.dma_start(wgs_t[:, 0:HALF], wgs[:, 0:HALF])
+        nc.sync.dma_start(wgs_t[:, 0:256], wgs[:, 0:256])
         pages = [load_rows(page0, 0, "page0_")]
-        nc.sync.dma_start(wgs_t[:, HALF:S], wgs[:, HALF:S])
+        nc.sync.dma_start(wgs_t[:, 256:S], wgs[:, 256:S])
 
         ident_bf = keep.tile([P, P], BF16, name="ident_bf")
         make_identity(nc, ident_bf[:])
@@ -248,7 +248,7 @@ def tile_list_saddle_reflocking_page_kernel(
                 rhs=codes[:].bitcast(FP8X4), rhs_scale=scales[:], start=True, stop=True,
             )
             nc.scalar.copy(out=y1, in_=y1_acc)
-            nc.scalar.activation(out=y2, in_=y2_acc, func=ACT.Identity, bias=1.0)
+            nc.vector.scalar_tensor_tensor(out=y2, in0=y2_acc, scalar=1.0, in1=y1, op0=ALU.add, op1=ALU.mult)
 
         def narrow_products(n, x_q, y1, y2):
             acc = psum.tile([P, 2, 256], F32, name="y_acc", tag="bank")
@@ -259,24 +259,20 @@ def tile_list_saddle_reflocking_page_kernel(
             acc2 = psum.tile([P, 512], F32, name="y2_acc", tag="bank")
             products(n, x_q, acc1[:], acc2[:], y1, y2)
 
-        def combine(y1, y2, start, count):
-            nc.gpsimd.tensor_tensor(y1, y1, wgo_t[:, start : start + count], ALU.mult)
-            nc.gpsimd.tensor_tensor(y2, y1, y2, ALU.mult)
-
         def put(n, y, start, count):
-            nc.vector.tensor_copy(outs[n][:].indirect(entries(list4, start, count)), y[:])
+            nc.vector.tensor_tensor(
+                outs[n][:].indirect(entries(list4, start, count)), y[:], wgo_t[:, start : start + count], ALU.mult
+            )
 
         def scores(n, x_q, start, y1, tag):
             y2 = keep.tile([P, 256], F32, name="y2", tag=tag, align_bytes=64)
             narrow_products(n, x_q, y1, y2[:])
-            combine(y1, y2[:], start, 256)
             return y2
 
         def wide_scores(n, x_q):
             y1 = ring.tile([P, HALF], F32, name="y1_wide", tag="raw", bufs=3)
             y2 = ring.tile([P, HALF], F32, name="y2_wide", tag="y2_wide", bufs=3)
             wide_products(n, x_q, y1[:], y2[:])
-            combine(y1[:], y2[:], HALF, HALF)
             return y2
 
         y1_first = keep.tile([P, N_TILES, 256], F32, name="y1_first", tag="h0")
@@ -307,6 +303,9 @@ def tile_list_saddle_reflocking_page_kernel(
         x_end = quantize_x(grouped_end, HALF, "x_end")
         for n in range(1, N_TILES):
             put(n, ys[n], FIRST, 256)
+        ys = [wide_scores(0, x_end)]
         for n in range(N_TILES):
-            put(n, wide_scores(n, x_end), HALF, HALF)
+            if n + 1 < N_TILES:
+                ys.append(wide_scores(n + 1, x_end))
+            put(n, ys[n], HALF, HALF)
             nc.sync.dma_start(out[n * P : (n + 1) * P, :], outs[n][:])

@@ -234,7 +234,7 @@ def tile_list_saddle_reflocking_page_kernel(
         x_first = quantize_x(grouped_first, FIRST, "x_first")
         picked_rest.extend(pick_rest(2, "hold_b", 64))
 
-        def products(n, x_q, y1_acc, y2_acc, y1, y2):
+        def products(n, x_q, y1_acc, y2_acc, y1):
             codes, scales = x_q
             w3_codes, w3_scales = w3_q[n // 2]
             rows = slice((n % 2) * P, (n % 2 + 1) * P)
@@ -248,21 +248,27 @@ def tile_list_saddle_reflocking_page_kernel(
                 rhs=codes[:].bitcast(FP8X4), rhs_scale=scales[:], start=True, stop=True,
             )
             nc.scalar.copy(out=y1, in_=y1_acc)
-            nc.vector.scalar_tensor_tensor(out=y2, in0=y2_acc, scalar=1.0, in1=y1, op0=ALU.add, op1=ALU.mult)
 
         def narrow_products(n, x_q, y1, y2):
             acc = psum.tile([P, 2, 256], F32, name="y_acc", tag="bank")
-            products(n, x_q, acc[:, 0, :], acc[:, 1, :], y1, y2)
+            products(n, x_q, acc[:, 0, :], acc[:, 1, :], y1)
+            nc.vector.scalar_tensor_tensor(out=y2, in0=acc[:, 1, :], scalar=1.0, in1=y1, op0=ALU.add, op1=ALU.mult)
 
         def wide_products(n, x_q, y1, y2):
             acc1 = psum.tile([P, 512], F32, name="y1_acc", tag="bank")
             acc2 = psum.tile([P, 512], F32, name="y2_acc", tag="bank")
-            products(n, x_q, acc1[:], acc2[:], y1, y2)
+            products(n, x_q, acc1[:], acc2[:], y1)
+            nc.scalar.activation(out=y2, in_=acc2[:], func=ACT.Identity, bias=1.0)
+            nc.gpsimd.tensor_tensor(y1, y1, wgo_t[:, HALF:S], ALU.mult)
+            nc.gpsimd.tensor_tensor(y2, y1, y2, ALU.mult)
 
         def put(n, y, start, count):
             nc.vector.tensor_tensor(
                 outs[n][:].indirect(entries(list4, start, count)), y[:], wgo_t[:, start : start + count], ALU.mult
             )
+
+        def put_weighted(n, y, start, count):
+            nc.vector.tensor_copy(outs[n][:].indirect(entries(list4, start, count)), y)
 
         def scores(n, x_q, start, y1, tag):
             y2 = keep.tile([P, 256], F32, name="y2", tag=tag, align_bytes=64)
@@ -295,17 +301,21 @@ def tile_list_saddle_reflocking_page_kernel(
         x_t_end = keep.tile([P, 4, H], BF16, name="x_t_end")
         for u in range(H_TILES):
             turn_in(picked_rest[u][:, 256:REST], u, 4, x_bf_rest[:, u, 256:REST], x_t_end)
-        grouped_end = keep.tile([P, 4 * 512], BF16, name="grouped_end", align_bytes=64)
+        grouped_end = keep.tile([P, 4 * 512], BF16, name="grouped_end", tag="hold_e", align_bytes=64)
         turn_back(x_t_end, 0, grouped_end, 0)
         turn_back(x_t_end, 2, grouped_end, 256)
         ys.extend(scores(n, x_mid, FIRST, y1_mid[:, n, :], "mid%d" % n) for n in range(2, N_TILES))
         put(0, ys[0], FIRST, 256)
         x_end = quantize_x(grouped_end, HALF, "x_end")
-        for n in range(1, N_TILES):
-            put(n, ys[n], FIRST, 256)
+        put(1, ys[1], FIRST, 256)
+        weighted = keep.tile([P, N_TILES - 2, 256], F32, name="weighted", tag="hold_e", align_bytes=64)
+        for n in range(2, N_TILES):
+            nc.vector.tensor_tensor(weighted[:, n - 2, :], ys[n][:], wgo_t[:, FIRST:HALF], ALU.mult)
+        for n in range(2, N_TILES):
+            put_weighted(n, weighted[:, n - 2, :], FIRST, 256)
         ys = [wide_scores(0, x_end)]
         for n in range(N_TILES):
             if n + 1 < N_TILES:
                 ys.append(wide_scores(n + 1, x_end))
-            put(n, ys[n], HALF, HALF)
+            put_weighted(n, ys[n][:], HALF, HALF)
             nc.sync.dma_start(out[n * P : (n + 1) * P, :], outs[n][:])

from contextlib import ExitStack

import concourse.mybir as mybir
from concourse.masks import make_identity

K, T, S, H, N = 1536, 2048, 1024, 512, 640
FLOPS = 2 * K * H * S + 2 * 2 * H * N * S

F32 = mybir.dt.float32
BF16 = mybir.dt.bfloat16
I32 = mybir.dt.int32
U32 = mybir.dt.uint32
U16 = mybir.dt.uint16
U8 = mybir.dt.uint8
FP8X4 = mybir.dt.float8_e4m3fn_x4
FP4X4 = mybir.dt.float4_e2m1fn_x4
ACT = mybir.ActivationFunctionType
ALU = mybir.AluOpType

P = 128
PASSES = K // 512
HALF = S // 2
FIRST = 256
REST = S - FIRST
H_TILES = H // P
N_TILES = N // P


def tile_list_saddle_reflocking_page_kernel(
    tc, tab_words, tab_scales, offs, offs2, offs3, offs4, w1, rest, wgs, page0, gain,
    w2_words, w2_scales, w3, wgo, page1, out,
):
    nc = tc.nc
    with ExitStack() as ctx:
        lists = ctx.enter_context(tc.tile_pool(name="lists", bufs=1))
        keep = ctx.enter_context(tc.tile_pool(name="keep", bufs=1))
        ring = ctx.enter_context(tc.tile_pool(name="ring", bufs=2))
        psum = ctx.enter_context(tc.psum_pool(name="psum", bufs=6))
        side = ctx.enter_context(tc.psum_pool(name="side", bufs=2))

        def load_list(src, name):
            tile = lists.tile([P, S // 16], U16, name=name)
            nc.sync.dma_start(tile[:], src)
            return tile

        def entries(tile, start, count):
            return tile[:, start // 16 : (start + count) // 16]

        def load_table_pass(a):
            tile = keep.tile([P, T], U32, name="tab_w%d" % a)
            nc.sync.dma_start(tile[:].bitcast(I32), tab_words[a].rearrange("p t i -> p (t i)").bitcast(I32))
            return tile

        def load_weight(src, row0, col0, width):
            raw = ring.tile([P, 4, width], F32, name="raw", tag="raw", bufs=3)
            nc.sync.dma_start(raw[:], src[row0 : row0 + 512, col0 : col0 + width].rearrange("(p i) c -> p i c", i=4))
            return raw

        def quantize_weight(raw, width, name):
            grouped = ring.tile([P, width, 4], BF16, name="w_bf", tag="w_bf", bufs=3, align_bytes=64)
            nc.scalar.copy(
                out=grouped[:].rearrange("p (c j) i -> p c i j", j=4),
                in_=raw[:, :, 0:width].rearrange("p i (c j) -> p c i j", j=4),
            )
            codes = keep.tile([P, width], U32, name=name + "_c", align_bytes=64)
            scales = keep.tile([P, width], U8, name=name + "_s", align_bytes=64)
            nc.vector.quantize_mx(
                out=codes[:].bitcast(FP8X4), scales=scales[:], in_=grouped[:].rearrange("p c i -> p (c i)")
            )
            return codes, scales

        def quantize_w1(raws, u):
            grouped = ring.tile([P, PASSES, P, 4], BF16, name="w1_bf", tag="w_bf", bufs=3, align_bytes=64)
            for a in range(PASSES):
                nc.scalar.copy(
                    out=grouped[:, a].rearrange("p (c j) i -> p c i j", j=4),
                    in_=raws[a][:, :, (u % 2) * P : (u % 2 + 1) * P].rearrange("p i (c j) -> p c i j", j=4),
                )
            codes = keep.tile([P, PASSES * P], U32, name="w1_c%d" % u, align_bytes=64)
            scales = keep.tile([P, PASSES * P], U8, name="w1_s%d" % u, align_bytes=64)
            nc.vector.quantize_mx(
                out=codes[:].bitcast(FP8X4), scales=scales[:], in_=grouped[:].rearrange("p a c i -> p (a c i)")
            )
            return [(codes[:, a * P : (a + 1) * P], scales[:, a * P : (a + 1) * P]) for a in range(PASSES)]

        def load_rows(src, u, name):
            tile = keep.tile([P, T], F32, name="%s%d" % (name, u))
            nc.sync.dma_start(tile[:], src[u * P : (u + 1) * P, :])
            return tile

        def load_cols(src, start, count, name):
            tile = keep.tile([P, count], F32, name=name)
            nc.sync.dma_start(tile[:], src[:, start : start + count])
            return tile

        tab_s = keep.tile([P, T], U8, name="tab_s")
        nc.vector.memset(tab_s[:].bitcast(I32), 0)
        w2_s = keep.tile([P, N], U8, name="w2_s", align_bytes=64)
        nc.vector.memset(w2_s[:].bitcast(I32), 0)
        list1 = load_list(offs, "list1")
        tab_w = [load_table_pass(0)]
        for q in range(4):
            nc.scalar.dma_start(
                tab_s[32 * q : 32 * q + 4 * PASSES, :].bitcast(I32), tab_scales[:, 4 * q : 4 * q + 4, :].bitcast(I32)
            )
        vectors = keep.tile([P, P], F32, name="vectors")
        nc.gpsimd.memset(vectors[:], 0.0)
        nc.scalar.dma_start(vectors[0:H_TILES, :], rest.rearrange("(u p) -> u p", p=P))
        nc.scalar.dma_start(vectors[H_TILES : 2 * H_TILES, :], gain.rearrange("(u p) -> u p", p=P))
        tab_w.extend(load_table_pass(a) for a in range(1, PASSES))
        w1_raw = [load_weight(w1, 512 * a, 0, 256) for a in range(PASSES)]
        list2 = load_list(offs2, "list2")
        wgs_t = keep.tile([P, S], F32, name="wgs_t", tag="hold_c")
        nc.sync.dma_start(wgs_t[:, 0:256], wgs[:, 0:256])
        pages = [load_rows(page0, 0, "page0_")]
        nc.sync.dma_start(wgs_t[:, 256:S], wgs[:, 256:S])

        ident_bf = keep.tile([P, P], BF16, name="ident_bf")
        make_identity(nc, ident_bf[:])
        ident_f32 = keep.tile([P, P], F32, name="ident_f32")
        make_identity(nc, ident_f32[:])
        warm = keep.tile([P, 1], F32, name="warm")
        nc.scalar.activation(out=warm[:], in_=ident_f32[:, 0:1], func=ACT.Sqrt, bias=1.0)

        turned_vectors = psum.tile([P, P], F32, name="turned_vectors", tag="bank")
        nc.tensor.transpose(turned_vectors[:], vectors[:], ident_f32[:])
        per_row = keep.tile([P, 2 * H_TILES], F32, name="per_row")
        nc.scalar.copy(out=per_row[:], in_=turned_vectors[:, 0 : 2 * H_TILES])

        got_w = [keep.tile([P, S], U32, name="got_w%d" % a, align_bytes=64) for a in range(PASSES)]
        got_s = keep.tile([P, S], U8, name="got_s", align_bytes=64)
        for a in range(PASSES):
            nc.vector.tensor_copy(got_w[a][:], tab_w[a][:].indirect(list1[:]))
        nc.vector.tensor_copy(got_s[:], tab_s[:].indirect(list1[:]))
        by_pass = [quantize_weight(w1_raw[a], P, "w1_first%d" % a) for a in range(PASSES)]
        w1_q = [[(codes[:], scales[:]) for codes, scales in by_pass], quantize_w1(w1_raw, 1)]

        w1_raw = [load_weight(w1, 512 * a, 256, 256) for a in range(PASSES)]
        list3 = load_list(offs3, "list3")
        pages.append(load_rows(page0, 1, "page0_"))

        def first_stage(u, start, count, h):
            cols = slice(start, start + count)
            acc = side.tile([P, count], F32, name="acc", tag="side")
            for a in range(PASSES):
                codes, scales = w1_q[u][a]
                nc.tensor.matmul_mx(
                    out=acc[:], lhsT=codes.bitcast(FP8X4), lhsT_scale=scales,
                    rhs=got_w[a][:, cols].bitcast(FP8X4), rhs_scale=got_s[4 * a : P, cols],
                    start=(a == 0), stop=(a == PASSES - 1),
                )
            square = ring.tile([P, count], F32, name="square", tag="square")
            nc.scalar.activation(out=square[:], in_=acc[:], func=ACT.Square, bias=per_row[:, u : u + 1], scale=-1.0)
            nc.scalar.activation(out=h[:, cols], in_=square[:], func=ACT.Sqrt, bias=1.0)

        def replace(u, h, start, count):
            cols = slice(start, start + count)
            nc.vector.tensor_tensor(
                pages[u][:].indirect(entries(list2, start, count)), h[:, cols], wgs_t[:, cols], ALU.mult
            )

        def turn_in(picked, u, blocks, x_bf, x_t):
            nc.scalar.activation(out=x_bf, in_=picked, func=ACT.Copy, scale=per_row[:, H_TILES + u : H_TILES + u + 1])
            turned = side.tile([P, blocks, P], BF16, name="turned", tag="side")
            for b in range(blocks):
                nc.tensor.transpose(turned[:, b, :], x_bf[:, b * P : (b + 1) * P], ident_bf[:])
            nc.scalar.copy(out=x_t[:, :, u * P : (u + 1) * P], in_=turned[:])

        def turn_back(x_t, b0, grouped, g0):
            words = x_t[:].bitcast(F32)
            back = side.tile([P, 2, 2, P], F32, name="back", tag="side")
            for b in range(2):
                for e in range(2):
                    nc.tensor.transpose(back[:, b, e, :], words[:, b0 + b, e : 2 * P : 2], ident_f32[:])
            nc.scalar.copy(
                out=grouped[:].bitcast(F32)[:, g0 * 2 : (g0 + 256) * 2].rearrange("p (b j e) -> p b j e", b=2, e=2),
                in_=back[:].rearrange("p b e j -> p b j e"),
            )

        def quantize_x(grouped, width, name):
            codes = keep.tile([P, width], U32, name=name + "_c", tag=name, align_bytes=64)
            scales = keep.tile([P, width], U8, name=name + "_s", align_bytes=64)
            nc.vector.quantize_mx(out=codes[:].bitcast(FP8X4), scales=scales[:], in_=grouped[:])
            return codes, scales

        hs = [
            keep.tile([P, S], F32, name="h%d" % u, tag="hold_a" if u == H_TILES - 1 else "h%d" % u)
            for u in range(H_TILES)
        ]
        for start, count in ((0, 256), (256, 256), (HALF, HALF)):
            first_stage(0, start, count, hs[0])
            replace(0, hs[0], start, count)
        for half in range(2):
            first_stage(1, half * HALF, HALF, hs[1])
        w1_q.extend(quantize_w1(w1_raw, u) for u in range(2, H_TILES))
        w3_cols = [(0, 256), (256, 256), (512, 128)]
        pages.append(load_rows(page0, 2, "page0_"))
        w3_raw = [load_weight(w3, 0, c0, width) for c0, width in w3_cols]
        pages.append(load_rows(page0, 3, "page0_"))
        w2_w = keep.tile([P, 2 * N], U8, name="w2_w", align_bytes=64)
        nc.sync.dma_start(w2_w[:].bitcast(I32), w2_words[0].bitcast(I32))
        for q in range(4):
            nc.sync.dma_start(
                w2_s[32 * q : 32 * q + 4, :].bitcast(I32), w2_scales[0, 4 * q : 4 * q + 4, :].bitcast(I32)
            )
        list4 = load_list(offs4, "list4")
        wgo_t = load_cols(wgo, 0, S, "wgo_t")
        outs = [load_rows(page1, n, "page1_") for n in range(N_TILES)]

        replace(1, hs[1], 0, S)
        for u in range(2, H_TILES):
            for half in range(2):
                first_stage(u, half * HALF, HALF, hs[u])
        replace(2, hs[2], 0, S)
        w3_q = [quantize_weight(w3_raw[i], w3_cols[i][1], "w3_%d" % i) for i in range(len(w3_cols))]
        replace(3, hs[3], 0, S)

        picked_first = keep.tile([P, H_TILES, FIRST], F32, name="picked_first", tag="hold_a")
        x_t_first = keep.tile([P, FIRST // P, H], BF16, name="x_t_first", tag="hold_d")
        for u in range(H_TILES):
            nc.vector.tensor_copy(picked_first[:, u, :], pages[u][:].indirect(entries(list3, 0, FIRST)))
            x_bf = ring.tile([P, FIRST], BF16, name="x_bf", tag="x_bf")
            turn_in(picked_first[:, u, :], u, FIRST // P, x_bf[:], x_t_first)
        grouped_first = keep.tile([P, 4 * FIRST], BF16, name="grouped_first", tag="hold_b", align_bytes=64)
        turn_back(x_t_first, 0, grouped_first, 0)

        def pick_rest(u0, tag, align):
            picked = keep.tile([P, 2, REST], F32, name="picked_rest%d" % u0, tag=tag, align_bytes=align)
            for i in range(2):
                nc.vector.tensor_copy(picked[:, i, :], pages[u0 + i][:].indirect(entries(list3, FIRST, REST)))
            return [picked[:, i, :] for i in range(2)]

        picked_rest = pick_rest(0, "hold_c", None)
        x_first = quantize_x(grouped_first, FIRST, "x_first")
        picked_rest.extend(pick_rest(2, "hold_b", 64))

        def products(n, x_q, y1_acc, y2_acc, y1):
            codes, scales = x_q
            w3_codes, w3_scales = w3_q[n // 2]
            rows = slice((n % 2) * P, (n % 2 + 1) * P)
            nc.tensor.matmul_mx(
                out=y1_acc, lhsT=w2_w[:, 2 * n * P : 2 * (n + 1) * P].bitcast(FP4X4),
                lhsT_scale=w2_s[:, n * P : (n + 1) * P],
                rhs=codes[:].bitcast(FP8X4), rhs_scale=scales[:], start=True, stop=True,
            )
            nc.tensor.matmul_mx(
                out=y2_acc, lhsT=w3_codes[:, rows].bitcast(FP8X4), lhsT_scale=w3_scales[:, rows],
                rhs=codes[:].bitcast(FP8X4), rhs_scale=scales[:], start=True, stop=True,
            )
            nc.scalar.copy(out=y1, in_=y1_acc)

        def narrow_products(n, x_q, y1, y2):
            acc = psum.tile([P, 2, 256], F32, name="y_acc", tag="bank")
            products(n, x_q, acc[:, 0, :], acc[:, 1, :], y1)
            nc.vector.scalar_tensor_tensor(out=y2, in0=acc[:, 1, :], scalar=1.0, in1=y1, op0=ALU.add, op1=ALU.mult)

        def wide_products(n, x_q, y1, y2):
            acc1 = psum.tile([P, 512], F32, name="y1_acc", tag="bank")
            acc2 = psum.tile([P, 512], F32, name="y2_acc", tag="bank")
            products(n, x_q, acc1[:], acc2[:], y1)
            nc.scalar.activation(out=y2, in_=acc2[:], func=ACT.Identity, bias=1.0)
            nc.gpsimd.tensor_tensor(y1, y1, wgo_t[:, HALF:S], ALU.mult)
            nc.gpsimd.tensor_tensor(y2, y1, y2, ALU.mult)

        def put(n, y, start, count):
            nc.vector.tensor_tensor(
                outs[n][:].indirect(entries(list4, start, count)), y[:], wgo_t[:, start : start + count], ALU.mult
            )

        def put_weighted(n, y, start, count):
            nc.vector.tensor_copy(outs[n][:].indirect(entries(list4, start, count)), y)

        def scores(n, x_q, start, y1, tag):
            y2 = keep.tile([P, 256], F32, name="y2", tag=tag, align_bytes=64)
            narrow_products(n, x_q, y1, y2[:])
            return y2

        def wide_scores(n, x_q):
            y1 = ring.tile([P, HALF], F32, name="y1_wide", tag="raw", bufs=3)
            y2 = ring.tile([P, HALF], F32, name="y2_wide", tag="y2_wide", bufs=3)
            wide_products(n, x_q, y1[:], y2[:])
            return y2

        y1_first = keep.tile([P, N_TILES, 256], F32, name="y1_first", tag="h0")
        y1_mid = keep.tile([P, N_TILES, 256], F32, name="y1_mid", tag="h1")

        ys = [scores(n, x_first, 0, y1_first[:, n, :], ("first0", "x_mid")[n]) for n in range(2)]
        x_bf_rest = keep.tile([P, H_TILES, REST], BF16, name="x_bf_rest", tag="hold_d")
        x_t_mid = keep.tile([P, 2, H], BF16, name="x_t_mid")
        for u in range(H_TILES):
            turn_in(picked_rest[u][:, 0:256], u, 2, x_bf_rest[:, u, 0:256], x_t_mid)
        grouped_mid = keep.tile([P, 4 * 256], BF16, name="grouped_mid", align_bytes=64)
        turn_back(x_t_mid, 0, grouped_mid, 0)
        ys.extend(scores(n, x_first, 0, y1_first[:, n, :], "first%d" % n) for n in range(2, N_TILES))
        for n in range(2):
            put(n, ys[n], 0, FIRST)
        x_mid = quantize_x(grouped_mid, 256, "x_mid")
        for n in range(2, N_TILES):
            put(n, ys[n], 0, FIRST)
        ys = [scores(n, x_mid, FIRST, y1_mid[:, n, :], ("x_end", "mid1")[n]) for n in range(2)]
        x_t_end = keep.tile([P, 4, H], BF16, name="x_t_end")
        for u in range(H_TILES):
            turn_in(picked_rest[u][:, 256:REST], u, 4, x_bf_rest[:, u, 256:REST], x_t_end)
        grouped_end = keep.tile([P, 4 * 512], BF16, name="grouped_end", tag="hold_e", align_bytes=64)
        turn_back(x_t_end, 0, grouped_end, 0)
        turn_back(x_t_end, 2, grouped_end, 256)
        ys.extend(scores(n, x_mid, FIRST, y1_mid[:, n, :], "mid%d" % n) for n in range(2, N_TILES))
        put(0, ys[0], FIRST, 256)
        x_end = quantize_x(grouped_end, HALF, "x_end")
        put(1, ys[1], FIRST, 256)
        weighted = keep.tile([P, N_TILES - 2, 256], F32, name="weighted", tag="hold_e", align_bytes=64)
        for n in range(2, N_TILES):
            nc.vector.tensor_tensor(weighted[:, n - 2, :], ys[n][:], wgo_t[:, FIRST:HALF], ALU.mult)
        for n in range(2, N_TILES):
            put_weighted(n, weighted[:, n - 2, :], FIRST, 256)
        ys = [wide_scores(0, x_end)]
        for n in range(N_TILES):
            if n + 1 < N_TILES:
                ys.append(wide_scores(n + 1, x_end))
            put_weighted(n, ys[n][:], HALF, HALF)
            nc.sync.dma_start(out[n * P : (n + 1) * P, :], outs[n][:])
